import numpy as np
import ml_dtypes


def mxq(x, axis, fmt="e4m3"):
    dtype, down = {"e4m3": (ml_dtypes.float8_e4m3fn, 7), "e5m2": (ml_dtypes.float8_e5m2, 14)}[fmt]
    v = np.moveaxis(np.asarray(x, np.float32).astype(ml_dtypes.bfloat16).astype(np.float64), axis, -1)
    blocks = v.reshape(v.shape[:-1] + (-1, 32))
    amax = np.abs(blocks).max(-1, keepdims=True)
    byte = np.maximum(np.where(amax > 0, np.frexp(amax)[1] - 1 + 127, 0) - down, 1)
    scale = np.exp2(byte - 127.0)
    codes = (blocks / scale).astype(np.float32).astype(dtype).astype(np.float64)
    return np.moveaxis((codes * scale).reshape(v.shape), -1, axis)


WIDE = False


def mx_kscale(k):
    if not WIDE:
        return np.ones(k)
    levels = np.array([10, -10, 5, -5, 0])
    if k % 512:
        return np.exp2(np.random.permutation(np.resize(levels, k // 32))).repeat(32)
    a = np.empty((k // 512, 16))
    for p in range(k // 512):
        a[p, :8] = np.random.permutation(np.resize(levels, 8))
        for g in range(8):
            far = levels[np.abs(levels - a[p, g]) >= 10]
            a[p, g + 8] = far[np.random.randint(len(far))]
    return np.exp2(a.ravel()).repeat(32)


def f64(x):
    return np.asarray(x).astype(np.float64)


def striped(idx):
    return np.tile(np.asarray(idx).reshape(-1, 16).T, (8, 1)).astype(np.uint16)


def unstriped(offs):
    return offs[:16].T.reshape(-1).astype(np.int64)


E2M1 = np.array([0.0, 0.5, 1.0, 1.5, 2.0, 3.0, 4.0, 6.0, -0.0, -0.5, -1.0, -1.5, -2.0, -3.0, -4.0, -6.0])


def pack_weight(w, fmt):
    k, n = w.shape
    w = f64(np.asarray(w, np.float32).astype(ml_dtypes.bfloat16)).reshape(k // 32, 32, n)
    amax = np.abs(w).max(1)
    if fmt == "e4m3":
        byte = np.frexp(amax)[1] - 1 + 127 - 7
    else:
        mant, ex = np.frexp(amax / 6.0)
        byte = np.where(mant > 0.5, ex, ex - 1) + 127
    byte = np.clip(np.where(amax > 0, byte, 1), 1, 254)
    scaled = (w * np.exp2(127.0 - byte)[:, None, :]).reshape(k, n).astype(np.float32)
    by_word = np.ascontiguousarray(scaled.reshape(k // 512, 128, 4, n).transpose(0, 1, 3, 2))
    if fmt == "e4m3":
        words = by_word.astype(ml_dtypes.float8_e4m3fn).view(np.uint8)
    else:
        c = by_word.astype(ml_dtypes.float4_e2m1fn).view(np.uint8) & 0xF
        words = (c[..., 0::2] | (c[..., 1::2] << 4)).reshape(k // 512, 128, 2 * n)
    return np.ascontiguousarray(words), np.ascontiguousarray(byte.astype(np.uint8).reshape(k // 512, 16, n))


def unpack_weight(words, scales, fmt):
    g, _, n = scales.shape
    words = np.ascontiguousarray(words).reshape(g, 128, n, -1)
    if fmt == "e4m3":
        vals = words.view(ml_dtypes.float8_e4m3fn).astype(np.float64)
    else:
        nib = np.empty((g, 128, n, 4), np.uint8)
        nib[..., 0::2] = words & 0xF
        nib[..., 1::2] = words >> 4
        vals = E2M1[nib]
    vals = vals * np.repeat(np.exp2(scales.astype(np.float64) - 127.0), 8, axis=1)[..., None]
    return vals.transpose(0, 1, 3, 2).reshape(g * 512, n)


D, T, I, Q, Z, M = 512, 2048, 512, 128, 1024, 2048


def setup_inputs():
    n = np.random.standard_normal
    idx = np.random.permutation(T)[:I]
    idx2 = np.random.permutation(Z)[:I]
    idx3 = np.random.permutation(Z)[:I]
    idx4 = np.random.permutation(M)[:I]
    fd = mx_kscale(D)
    keysp = pack_weight(n((D, T)) / fd[:, None], "e2m1")
    return {
        "query": (n((D, Q)) * 1.0 / np.sqrt(D) * fd[:, None]).astype(np.float32),
        "query2": (n((D, Q)) * 1.0 / np.sqrt(D) * fd[:, None]).astype(np.float32),
        "keys_words": keysp[0],
        "keys_scales": keysp[1],
        "pages": (n((D, Z)) / fd[:, None]).astype(np.float32),
        "old": (np.random.uniform(0.0, 2.0, (Q, M))).astype(np.float32),
        "fade": (np.random.uniform(0.3, 0.9, (Q, 1))).astype(np.float32),
        "offs": striped(idx),
        "offs2": striped(idx2),
        "offs3": striped(idx3),
        "offs4": striped(idx4),
    }


def reference(query, query2, keys_words, keys_scales, pages, old, fade, offs, offs2, offs3, offs4):
    idx = unstriped(offs)
    idx2 = unstriped(offs2)
    idx3 = unstriped(offs3)
    idx4 = unstriped(offs4)
    keysu = unpack_weight(keys_words, keys_scales, "e2m1")
    queryq = mxq(f64(query), 0, "e4m3")
    a = queryq.T @ keysu
    query2q = mxq(f64(query2), 0, "e4m3")
    pagesq = mxq(f64(pages), 0, "e4m3")
    h0 = query2q.T @ pagesq
    s = np.maximum(a[:, idx], h0[:, idx2]) - h0[:, idx3]
    w = np.maximum(s, 0.0)
    ws = w * 2.0
    wf = np.zeros((Q, M))
    wf[:, idx4] = ws
    y = f64(old) * f64(fade) + wf
    return y

@@ -1,0 +1,128 @@
+from contextlib import ExitStack
+
+import concourse.mybir as mybir
+
+D, T, I, Q, Z, M = 512, 2048, 512, 128, 1024, 2048
+FLOPS = 2 * D * Q * (T + Z)
+
+F32 = mybir.dt.float32
+BF16 = mybir.dt.bfloat16
+I32 = mybir.dt.int32
+U32 = mybir.dt.uint32
+U16 = mybir.dt.uint16
+U8 = mybir.dt.uint8
+FP8X4 = mybir.dt.float8_e4m3fn_x4
+FP4X4 = mybir.dt.float4_e2m1fn_x4
+ALU = mybir.AluOpType
+COPY = mybir.ActivationFunctionType.Copy
+
+P = 128
+PACK = 4
+BANK = 512
+PAGE_CHUNKS = (256, 256, 256, 128, 128)
+STORE_CHUNKS = (256, 512, 512, 512, 256)
+HALF = I // 2
+PIECE = 128
+
+
+def starts(widths):
+    return [sum(widths[:n]) for n in range(len(widths))]
+
+
+def tile_attend_largestof3_counts_lean_kernel(tc, query, query2, keys_words, keys_scales, pages, old, fade,
+                                               offs, offs2, offs3, offs4, out):
+    nc = tc.nc
+    with ExitStack() as ctx:
+        lists = ctx.enter_context(tc.tile_pool(name="lists", bufs=1))
+        keep = ctx.enter_context(tc.tile_pool(name="keep", bufs=1))
+        psum = ctx.enter_context(tc.psum_pool(name="psum", bufs=8))
+
+        def load_rows(name, rows):
+            raw = keep.tile([P, PACK, rows.shape[1]], F32, name=name)
+            nc.sync.dma_start(out=raw[:], in_=rows.rearrange("(p j) w -> p j w", j=PACK))
+            return raw
+
+        def load_list(name, src):
+            t = lists.tile([P, I // 16], U16, name=name)
+            nc.sync.dma_start(t[:], src)
+            return t
+
+        def quantize(name, raw):
+            width = raw.shape[2]
+            grouped = keep.tile([P, width * PACK], BF16, name=name + "_bf", align_bytes=64)
+            nc.vector.tensor_copy(
+                out=grouped[:].rearrange("p (c i t) -> p c t i", i=4, t=PACK),
+                in_=raw[:].rearrange("p t (c i) -> p c t i", i=4),
+            )
+            codes = keep.tile([P, width], U32, name=name + "_codes", align_bytes=64)
+            scales = keep.tile([P, width], U8, name=name + "_scales", align_bytes=64)
+            nc.vector.quantize_mx(out=codes[:].bitcast(FP8X4), scales=scales[:], in_=grouped[:])
+            return codes, scales
+
+        key_scales = keep.tile([P, T], U8, name="key_scales", align_bytes=64)
+        nc.vector.memset(key_scales[:].bitcast(I32), 0)
+        placed = keep.tile([P, M], F32, name="placed")
+        nc.vector.memset(placed[:], 0.0)
+
+        query_raw = load_rows("query_raw", query)
+        key_words = keep.tile([P, 2 * T], U8, name="key_words", align_bytes=64)
+        nc.sync.dma_start(out=key_words[:].bitcast(I32), in_=keys_words[0].bitcast(I32))
+        for quad in range(4):
+            nc.scalar.dma_start(out=key_scales[32 * quad:32 * quad + 4, :].bitcast(I32),
+                                in_=keys_scales[0, 4 * quad:4 * quad + 4, :].bitcast(I32))
+        token_list = load_list("token_list", offs)
+        query2_raw = load_rows("query2_raw", query2)
+        page_raw = [load_rows("page_raw%d" % n, pages[:, z0:z0 + w])
+                    for n, (z0, w) in enumerate(zip(starts(PAGE_CHUNKS), PAGE_CHUNKS))]
+        plus_list = load_list("plus_list", offs2)
+        minus_list = load_list("minus_list", offs3)
+        place_list = load_list("place_list", offs4)
+        fade_col = keep.tile([P, 1], F32, name="fade_col")
+        nc.sync.dma_start(out=fade_col[:], in_=fade)
+        old_sb = keep.tile([P, M], F32, name="old_sb")
+        nc.sync.dma_start(out=old_sb[:], in_=old)
+
+        q_codes, q_scales = quantize("query", query_raw)
+        a_sb = keep.tile([P, T], F32, name="a_sb")
+        for t0 in range(0, T, BANK):
+            acc = psum.tile([P, BANK], F32, name="acc")
+            nc.tensor.matmul_mx(out=acc[:], lhsT=q_codes[:].bitcast(FP8X4), lhsT_scale=q_scales[:],
+                                rhs=key_words[:, 2 * t0:2 * (t0 + BANK)].bitcast(FP4X4),
+                                rhs_scale=key_scales[:, t0:t0 + BANK], start=True, stop=True)
+            nc.scalar.activation(a_sb[:, t0:t0 + BANK], acc[:], COPY)
+        a_listed = keep.tile([P, I], F32, name="a_listed")
+        nc.scalar.activation(a_listed[:], a_sb[:].indirect(token_list[:]), COPY)
+
+        q2_codes, q2_scales = quantize("query2", query2_raw)
+        h_sb = keep.tile([P, Z], F32, name="h_sb")
+        for n, (z0, w) in enumerate(zip(starts(PAGE_CHUNKS), PAGE_CHUNKS)):
+            codes, scales = quantize("page%d" % n, page_raw[n])
+            acc = psum.tile([P, BANK], F32, name="acc")
+            nc.tensor.matmul_mx(out=acc[:, 0:w], lhsT=q2_codes[:].bitcast(FP8X4), lhsT_scale=q2_scales[:],
+                                rhs=codes[:].bitcast(FP8X4), rhs_scale=scales[:], start=True, stop=True)
+            nc.scalar.activation(h_sb[:, z0:z0 + w], acc[:, 0:w], COPY)
+
+        score = keep.tile([P, HALF], F32, name="score")
+        h_minus = keep.tile([P, I], F32, name="h_minus")
+        weight = keep.tile([P, I], F32, name="weight")
+        for i0 in range(0, I, HALF):
+            nc.scalar.activation(h_minus[:, i0:i0 + HALF],
+                                 h_sb[:].indirect(minus_list[:, i0 // 16:(i0 + HALF) // 16]), COPY)
+        for i0 in range(0, I, HALF):
+            pieces = [(slice(s0, s0 + PIECE), slice(i0 + s0, i0 + s0 + PIECE)) for s0 in range(0, HALF, PIECE)]
+            for c, s in pieces:
+                nc.vector.tensor_copy(score[:, c], h_sb[:].indirect(plus_list[:, s.start // 16:s.stop // 16]))
+            for c, s in pieces:
+                nc.vector.tensor_tensor(score[:, c], score[:, c], a_listed[:, s], ALU.max)
+            for c, s in pieces:
+                nc.vector.tensor_tensor(score[:, c], score[:, c], h_minus[:, s], ALU.subtract)
+            for c, s in pieces:
+                nc.vector.tensor_scalar(weight[:, s], score[:, c], 0.0, 2.0, ALU.max, ALU.mult)
+            nc.scalar.activation(placed[:].indirect(place_list[:, i0 // 16:(i0 + HALF) // 16]),
+                                 weight[:, i0:i0 + HALF], COPY)
+
+        for n, (m0, w) in enumerate(zip(starts(STORE_CHUNKS), STORE_CHUNKS)):
+            result = keep.tile([P, w], F32, name="result%d" % n)
+            nc.vector.scalar_tensor_tensor(result[:], old_sb[:, m0:m0 + w], fade_col[:], placed[:, m0:m0 + w],
+                                           ALU.mult, ALU.add)
+            nc.sync.dma_start(out=out[:, m0:m0 + w], in_=result[:])

@@ -19,7 +19,9 @@ COPY = mybir.ActivationFunctionType.Copy
 P = 128
 PACK = 4
 BANK = 512
-PAGE_CHUNKS = (256, 256, 256, 128, 128)
+PAGE_CHUNKS = (384, 384, 256)
+PAGE_UNITS = ((128, 256), (256, 128), (128, 128))
+SCALAR_UNIT = (2, 1)
 STORE_CHUNKS = (256, 512, 512, 512, 256)
 HALF = I // 2
 PIECE = 128
@@ -47,13 +49,15 @@ def tile_attend_largestof3_counts_lean_kernel(tc, query, query2, keys_words, key
             nc.sync.dma_start(t[:], src)
             return t
 
-        def quantize(name, raw):
+        def quantize(name, raw, on_scalar=False):
             width = raw.shape[2]
             grouped = keep.tile([P, width * PACK], BF16, name=name + "_bf", align_bytes=64)
-            nc.vector.tensor_copy(
-                out=grouped[:].rearrange("p (c i t) -> p c t i", i=4, t=PACK),
-                in_=raw[:].rearrange("p t (c i) -> p c t i", i=4),
-            )
+            dst = grouped[:].rearrange("p (c i t) -> p c t i", i=4, t=PACK)
+            src = raw.rearrange("p t (c i) -> p c t i", i=4)
+            if on_scalar:
+                nc.scalar.copy(out=dst, in_=src)
+            else:
+                nc.vector.tensor_copy(out=dst, in_=src)
             codes = keep.tile([P, width], U32, name=name + "_codes", align_bytes=64)
             scales = keep.tile([P, width], U8, name=name + "_scales", align_bytes=64)
             nc.vector.quantize_mx(out=codes[:].bitcast(FP8X4), scales=scales[:], in_=grouped[:])
@@ -67,13 +71,14 @@ def tile_attend_largestof3_counts_lean_kernel(tc, query, query2, keys_words, key
         query_raw = load_rows("query_raw", query)
         key_words = keep.tile([P, 2 * T], U8, name="key_words", align_bytes=64)
         nc.sync.dma_start(out=key_words[:].bitcast(I32), in_=keys_words[0].bitcast(I32))
-        for quad in range(4):
-            nc.scalar.dma_start(out=key_scales[32 * quad:32 * quad + 4, :].bitcast(I32),
-                                in_=keys_scales[0, 4 * quad:4 * quad + 4, :].bitcast(I32))
-        token_list = load_list("token_list", offs)
+        for r in range(4):
+            nc.sync.dma_start(out=key_scales[r:P:32, :].bitcast(I32), in_=keys_scales[0, r:16:4, :].bitcast(I32))
         query2_raw = load_rows("query2_raw", query2)
-        page_raw = [load_rows("page_raw%d" % n, pages[:, z0:z0 + w])
-                    for n, (z0, w) in enumerate(zip(starts(PAGE_CHUNKS), PAGE_CHUNKS))]
+        page_raw = []
+        for n, (z0, w) in enumerate(zip(starts(PAGE_CHUNKS), PAGE_CHUNKS)):
+            page_raw.append(load_rows("page_raw%d" % n, pages[:, z0:z0 + w]))
+            if n == 0:
+                token_list = load_list("token_list", offs)
         plus_list = load_list("plus_list", offs2)
         minus_list = load_list("minus_list", offs3)
         place_list = load_list("place_list", offs4)
@@ -82,8 +87,8 @@ def tile_attend_largestof3_counts_lean_kernel(tc, query, query2, keys_words, key
         old_sb = keep.tile([P, M], F32, name="old_sb")
         nc.sync.dma_start(out=old_sb[:], in_=old)
 
-        q_codes, q_scales = quantize("query", query_raw)
-        a_sb = keep.tile([P, T], F32, name="a_sb")
+        q_codes, q_scales = quantize("query", query_raw[:])
+        a_sb = keep.tile([P, T], F32, name="a_sb", tag="window")
         for t0 in range(0, T, BANK):
             acc = psum.tile([P, BANK], F32, name="acc")
             nc.tensor.matmul_mx(out=acc[:], lhsT=q_codes[:].bitcast(FP8X4), lhsT_scale=q_scales[:],
@@ -93,33 +98,43 @@ def tile_attend_largestof3_counts_lean_kernel(tc, query, query2, keys_words, key
         a_listed = keep.tile([P, I], F32, name="a_listed")
         nc.scalar.activation(a_listed[:], a_sb[:].indirect(token_list[:]), COPY)
 
-        q2_codes, q2_scales = quantize("query2", query2_raw)
-        h_sb = keep.tile([P, Z], F32, name="h_sb")
-        for n, (z0, w) in enumerate(zip(starts(PAGE_CHUNKS), PAGE_CHUNKS)):
-            codes, scales = quantize("page%d" % n, page_raw[n])
-            acc = psum.tile([P, BANK], F32, name="acc")
-            nc.tensor.matmul_mx(out=acc[:, 0:w], lhsT=q2_codes[:].bitcast(FP8X4), lhsT_scale=q2_scales[:],
-                                rhs=codes[:].bitcast(FP8X4), rhs_scale=scales[:], start=True, stop=True)
-            nc.scalar.activation(h_sb[:, z0:z0 + w], acc[:, 0:w], COPY)
+        q2_codes, q2_scales = quantize("query2", query2_raw[:])
+        h_sb = keep.tile([P, Z], F32, name="h_sb", tag="window")
+        for n, chunk0 in enumerate(starts(PAGE_CHUNKS)):
+            for u, (c0, w) in enumerate(zip(starts(PAGE_UNITS[n]), PAGE_UNITS[n])):
+                z0 = chunk0 + c0
+                codes, scales = quantize("page%d" % z0, page_raw[n][:, :, c0:c0 + w], (n, u) == SCALAR_UNIT)
+                acc = psum.tile([P, BANK], F32, name="acc")
+                nc.tensor.matmul_mx(out=acc[:, 0:w], lhsT=q2_codes[:].bitcast(FP8X4), lhsT_scale=q2_scales[:],
+                                    rhs=codes[:].bitcast(FP8X4), rhs_scale=scales[:], start=True, stop=True)
+                if n == 2:
+                    nc.vector.tensor_copy(h_sb[:, z0:z0 + w], acc[:, 0:w])
+                else:
+                    nc.scalar.activation(h_sb[:, z0:z0 + w], acc[:, 0:w], COPY)
 
-        score = keep.tile([P, HALF], F32, name="score")
         h_minus = keep.tile([P, I], F32, name="h_minus")
+        page_lead = keep.tile([P, HALF], F32, name="page_lead")
+        token_lead = keep.tile([P, HALF], F32, name="token_lead")
         weight = keep.tile([P, I], F32, name="weight")
-        for i0 in range(0, I, HALF):
-            nc.scalar.activation(h_minus[:, i0:i0 + HALF],
-                                 h_sb[:].indirect(minus_list[:, i0 // 16:(i0 + HALF) // 16]), COPY)
+
+        def entries(tile, s):
+            return tile[:, s.start // 16:s.stop // 16]
+
+        for s in (slice(0, PIECE), slice(PIECE, HALF), slice(HALF, I)):
+            nc.scalar.activation(h_minus[:, s], h_sb[:].indirect(entries(minus_list, s)), COPY)
         for i0 in range(0, I, HALF):
             pieces = [(slice(s0, s0 + PIECE), slice(i0 + s0, i0 + s0 + PIECE)) for s0 in range(0, HALF, PIECE)]
+            if i0 == 0:
+                for c, s in pieces:
+                    nc.vector.tensor_copy(page_lead[:, c], h_sb[:].indirect(entries(plus_list, s)))
             for c, s in pieces:
-                nc.vector.tensor_copy(score[:, c], h_sb[:].indirect(plus_list[:, s.start // 16:s.stop // 16]))
+                h_plus = page_lead[:, c] if i0 == 0 else h_sb[:].indirect(entries(plus_list, s))
+                nc.vector.tensor_tensor(token_lead[:, c], a_listed[:, s], h_minus[:, s], ALU.subtract)
+                nc.vector.tensor_tensor(page_lead[:, c], h_plus, h_minus[:, s], ALU.subtract)
             for c, s in pieces:
-                nc.vector.tensor_tensor(score[:, c], score[:, c], a_listed[:, s], ALU.max)
-            for c, s in pieces:
-                nc.vector.tensor_tensor(score[:, c], score[:, c], h_minus[:, s], ALU.subtract)
-            for c, s in pieces:
-                nc.vector.tensor_scalar(weight[:, s], score[:, c], 0.0, 2.0, ALU.max, ALU.mult)
-            nc.scalar.activation(placed[:].indirect(place_list[:, i0 // 16:(i0 + HALF) // 16]),
-                                 weight[:, i0:i0 + HALF], COPY)
+                nc.vector.scalar_tensor_tensor(weight[:, s], token_lead[:, c], 0.0, page_lead[:, c], ALU.max, ALU.max)
+            half = slice(i0, i0 + HALF)
+            nc.scalar.activation(placed[:].indirect(entries(place_list, half)), weight[:, half], COPY, scale=2.0)
 
         for n, (m0, w) in enumerate(zip(starts(STORE_CHUNKS), STORE_CHUNKS)):
             result = keep.tile([P, w], F32, name="result%d" % n)

from contextlib import ExitStack

import concourse.mybir as mybir

D, T, I, Q, Z, M = 512, 2048, 512, 128, 1024, 2048
FLOPS = 2 * D * Q * (T + Z)

F32 = mybir.dt.float32
BF16 = mybir.dt.bfloat16
I32 = mybir.dt.int32
U32 = mybir.dt.uint32
U16 = mybir.dt.uint16
U8 = mybir.dt.uint8
FP8X4 = mybir.dt.float8_e4m3fn_x4
FP4X4 = mybir.dt.float4_e2m1fn_x4
ALU = mybir.AluOpType
COPY = mybir.ActivationFunctionType.Copy

P = 128
PACK = 4
BANK = 512
PAGE_CHUNKS = (384, 384, 256)
PAGE_UNITS = ((128, 256), (256, 128), (128, 128))
SCALAR_UNIT = (2, 1)
STORE_CHUNKS = (256, 512, 512, 512, 256)
HALF = I // 2
PIECE = 128


def starts(widths):
    return [sum(widths[:n]) for n in range(len(widths))]


def tile_attend_largestof3_counts_lean_kernel(tc, query, query2, keys_words, keys_scales, pages, old, fade,
                                               offs, offs2, offs3, offs4, out):
    nc = tc.nc
    with ExitStack() as ctx:
        lists = ctx.enter_context(tc.tile_pool(name="lists", bufs=1))
        keep = ctx.enter_context(tc.tile_pool(name="keep", bufs=1))
        psum = ctx.enter_context(tc.psum_pool(name="psum", bufs=8))

        def load_rows(name, rows):
            raw = keep.tile([P, PACK, rows.shape[1]], F32, name=name)
            nc.sync.dma_start(out=raw[:], in_=rows.rearrange("(p j) w -> p j w", j=PACK))
            return raw

        def load_list(name, src):
            t = lists.tile([P, I // 16], U16, name=name)
            nc.sync.dma_start(t[:], src)
            return t

        def quantize(name, raw, on_scalar=False):
            width = raw.shape[2]
            grouped = keep.tile([P, width * PACK], BF16, name=name + "_bf", align_bytes=64)
            dst = grouped[:].rearrange("p (c i t) -> p c t i", i=4, t=PACK)
            src = raw.rearrange("p t (c i) -> p c t i", i=4)
            if on_scalar:
                nc.scalar.copy(out=dst, in_=src)
            else:
                nc.vector.tensor_copy(out=dst, in_=src)
            codes = keep.tile([P, width], U32, name=name + "_codes", align_bytes=64)
            scales = keep.tile([P, width], U8, name=name + "_scales", align_bytes=64)
            nc.vector.quantize_mx(out=codes[:].bitcast(FP8X4), scales=scales[:], in_=grouped[:])
            return codes, scales

        key_scales = keep.tile([P, T], U8, name="key_scales", align_bytes=64)
        nc.vector.memset(key_scales[:].bitcast(I32), 0)
        placed = keep.tile([P, M], F32, name="placed")
        nc.vector.memset(placed[:], 0.0)

        query_raw = load_rows("query_raw", query)
        key_words = keep.tile([P, 2 * T], U8, name="key_words", align_bytes=64)
        nc.sync.dma_start(out=key_words[:].bitcast(I32), in_=keys_words[0].bitcast(I32))
        for r in range(4):
            nc.sync.dma_start(out=key_scales[r:P:32, :].bitcast(I32), in_=keys_scales[0, r:16:4, :].bitcast(I32))
        query2_raw = load_rows("query2_raw", query2)
        page_raw = []
        for n, (z0, w) in enumerate(zip(starts(PAGE_CHUNKS), PAGE_CHUNKS)):
            page_raw.append(load_rows("page_raw%d" % n, pages[:, z0:z0 + w]))
            if n == 0:
                token_list = load_list("token_list", offs)
        plus_list = load_list("plus_list", offs2)
        minus_list = load_list("minus_list", offs3)
        place_list = load_list("place_list", offs4)
        fade_col = keep.tile([P, 1], F32, name="fade_col")
        nc.sync.dma_start(out=fade_col[:], in_=fade)
        old_sb = keep.tile([P, M], F32, name="old_sb")
        nc.sync.dma_start(out=old_sb[:], in_=old)

        q_codes, q_scales = quantize("query", query_raw[:])
        a_sb = keep.tile([P, T], F32, name="a_sb", tag="window")
        for t0 in range(0, T, BANK):
            acc = psum.tile([P, BANK], F32, name="acc")
            nc.tensor.matmul_mx(out=acc[:], lhsT=q_codes[:].bitcast(FP8X4), lhsT_scale=q_scales[:],
                                rhs=key_words[:, 2 * t0:2 * (t0 + BANK)].bitcast(FP4X4),
                                rhs_scale=key_scales[:, t0:t0 + BANK], start=True, stop=True)
            nc.scalar.activation(a_sb[:, t0:t0 + BANK], acc[:], COPY)
        a_listed = keep.tile([P, I], F32, name="a_listed")
        nc.scalar.activation(a_listed[:], a_sb[:].indirect(token_list[:]), COPY)

        q2_codes, q2_scales = quantize("query2", query2_raw[:])
        h_sb = keep.tile([P, Z], F32, name="h_sb", tag="window")
        for n, chunk0 in enumerate(starts(PAGE_CHUNKS)):
            for u, (c0, w) in enumerate(zip(starts(PAGE_UNITS[n]), PAGE_UNITS[n])):
                z0 = chunk0 + c0
                codes, scales = quantize("page%d" % z0, page_raw[n][:, :, c0:c0 + w], (n, u) == SCALAR_UNIT)
                acc = psum.tile([P, BANK], F32, name="acc")
                nc.tensor.matmul_mx(out=acc[:, 0:w], lhsT=q2_codes[:].bitcast(FP8X4), lhsT_scale=q2_scales[:],
                                    rhs=codes[:].bitcast(FP8X4), rhs_scale=scales[:], start=True, stop=True)
                if n == 2:
                    nc.vector.tensor_copy(h_sb[:, z0:z0 + w], acc[:, 0:w])
                else:
                    nc.scalar.activation(h_sb[:, z0:z0 + w], acc[:, 0:w], COPY)

        h_minus = keep.tile([P, I], F32, name="h_minus")
        page_lead = keep.tile([P, HALF], F32, name="page_lead")
        token_lead = keep.tile([P, HALF], F32, name="token_lead")
        weight = keep.tile([P, I], F32, name="weight")

        def entries(tile, s):
            return tile[:, s.start // 16:s.stop // 16]

        for s in (slice(0, PIECE), slice(PIECE, HALF), slice(HALF, I)):
            nc.scalar.activation(h_minus[:, s], h_sb[:].indirect(entries(minus_list, s)), COPY)
        for i0 in range(0, I, HALF):
            pieces = [(slice(s0, s0 + PIECE), slice(i0 + s0, i0 + s0 + PIECE)) for s0 in range(0, HALF, PIECE)]
            if i0 == 0:
                for c, s in pieces:
                    nc.vector.tensor_copy(page_lead[:, c], h_sb[:].indirect(entries(plus_list, s)))
            for c, s in pieces:
                h_plus = page_lead[:, c] if i0 == 0 else h_sb[:].indirect(entries(plus_list, s))
                nc.vector.tensor_tensor(token_lead[:, c], a_listed[:, s], h_minus[:, s], ALU.subtract)
                nc.vector.tensor_tensor(page_lead[:, c], h_plus, h_minus[:, s], ALU.subtract)
            for c, s in pieces:
                nc.vector.scalar_tensor_tensor(weight[:, s], token_lead[:, c], 0.0, page_lead[:, c], ALU.max, ALU.max)
            half = slice(i0, i0 + HALF)
            nc.scalar.activation(placed[:].indirect(entries(place_list, half)), weight[:, half], COPY, scale=2.0)

        for n, (m0, w) in enumerate(zip(starts(STORE_CHUNKS), STORE_CHUNKS)):
            result = keep.tile([P, w], F32, name="result%d" % n)
            nc.vector.scalar_tensor_tensor(result[:], old_sb[:, m0:m0 + w], fade_col[:], placed[:, m0:m0 + w],
                                           ALU.mult, ALU.add)
            nc.sync.dma_start(out=out[:, m0:m0 + w], in_=result[:])
